import numpy as np
import ml_dtypes


def mxq(x, axis, fmt="e4m3"):
    dtype, down = {"e4m3": (ml_dtypes.float8_e4m3fn, 7), "e5m2": (ml_dtypes.float8_e5m2, 14)}[fmt]
    v = np.moveaxis(np.asarray(x, np.float32).astype(ml_dtypes.bfloat16).astype(np.float64), axis, -1)
    blocks = v.reshape(v.shape[:-1] + (-1, 32))
    amax = np.abs(blocks).max(-1, keepdims=True)
    byte = np.maximum(np.where(amax > 0, np.frexp(amax)[1] - 1 + 127, 0) - down, 1)
    scale = np.exp2(byte - 127.0)
    codes = (blocks / scale).astype(np.float32).astype(dtype).astype(np.float64)
    return np.moveaxis((codes * scale).reshape(v.shape), -1, axis)


WIDE = False


def mx_kscale(k):
    if not WIDE:
        return np.ones(k)
    levels = np.array([10, -10, 5, -5, 0])
    if k % 512:
        return np.exp2(np.random.permutation(np.resize(levels, k // 32))).repeat(32)
    a = np.empty((k // 512, 16))
    for p in range(k // 512):
        a[p, :8] = np.random.permutation(np.resize(levels, 8))
        for g in range(8):
            far = levels[np.abs(levels - a[p, g]) >= 10]
            a[p, g + 8] = far[np.random.randint(len(far))]
    return np.exp2(a.ravel()).repeat(32)


def f64(x):
    return np.asarray(x).astype(np.float64)


def striped(idx):
    return np.tile(idx.reshape(-1, 16).T, (8, 1)).astype(np.uint16)


def unstriped(offs):
    return offs[:16].T.reshape(-1).astype(np.int64)


E2M1 = np.array([0.0, 0.5, 1.0, 1.5, 2.0, 3.0, 4.0, 6.0, -0.0, -0.5, -1.0, -1.5, -2.0, -3.0, -4.0, -6.0])


def pack_weight(w, fmt):
    k, n = w.shape
    w = f64(np.asarray(w, np.float32).astype(ml_dtypes.bfloat16)).reshape(k // 32, 32, n)
    amax = np.abs(w).max(1)
    if fmt == "e4m3":
        byte = np.frexp(amax)[1] - 1 + 127 - 7
    else:
        mant, ex = np.frexp(amax / 6.0)
        byte = np.where(mant > 0.5, ex, ex - 1) + 127
    byte = np.clip(np.where(amax > 0, byte, 1), 1, 254)
    scaled = (w * np.exp2(127.0 - byte)[:, None, :]).reshape(k, n).astype(np.float32)
    by_word = np.ascontiguousarray(scaled.reshape(k // 512, 128, 4, n).transpose(0, 1, 3, 2))
    if fmt == "e4m3":
        words = by_word.astype(ml_dtypes.float8_e4m3fn).view(np.uint8)
    else:
        c = by_word.astype(ml_dtypes.float4_e2m1fn).view(np.uint8) & 0xF
        words = (c[..., 0::2] | (c[..., 1::2] << 4)).reshape(k // 512, 128, 2 * n)
    return np.ascontiguousarray(words), np.ascontiguousarray(byte.astype(np.uint8).reshape(k // 512, 16, n))


def unpack_weight(words, scales, fmt):
    g, _, n = scales.shape
    words = np.ascontiguousarray(words).reshape(g, 128, n, -1)
    if fmt == "e4m3":
        vals = words.view(ml_dtypes.float8_e4m3fn).astype(np.float64)
    else:
        nib = np.empty((g, 128, n, 4), np.uint8)
        nib[..., 0::2] = words & 0xF
        nib[..., 1::2] = words >> 4
        vals = E2M1[nib]
    vals = vals * np.repeat(np.exp2(scales.astype(np.float64) - 127.0), 8, axis=1)[..., None]
    return vals.transpose(0, 1, 3, 2).reshape(g * 512, n)


def pack_table(v):
    words, scales = pack_weight(v, "e4m3")
    return np.concatenate([words.reshape(words.shape[0], -1), scales.reshape(scales.shape[0], -1)], axis=1)


def unpack_table(tab):
    g, t = tab.shape[0], tab.shape[1] // 528
    return unpack_weight(tab[:, :512 * t].reshape(g, 128, t, 4), tab[:, 512 * t:].reshape(g, 16, t), "e4m3")


K, M, T, S = 1024, 256, 4096, 512


def setup_inputs():
    n = np.random.standard_normal
    s = mx_kscale(K)[:, None]
    p_w0 = pack_weight(n((K, M)) / np.sqrt(3 * K) / s, "e2m1")
    p_w1 = pack_weight(n((K, M)) / np.sqrt(3 * K) / s, "e4m3")
    return {
        "tab": pack_table(n((K, T)) * s),
        "w0_words": p_w0[0],
        "w0_scales": p_w0[1],
        "w1_words": p_w1[0],
        "w1_scales": p_w1[1],
        "w2": (n((K, M)) / np.sqrt(3 * K) / s).astype(np.float32),
        "offs": striped(np.concatenate([np.random.permutation(T)[:S] for _ in range(3)])),
    }


def reference(tab, w0_words, w0_scales, w1_words, w1_scales, w2, offs):
    v = unpack_table(tab)
    idx = unstriped(offs).reshape(3, S)
    w0_ = unpack_weight(w0_words, w0_scales, "e2m1")
    w1_ = unpack_weight(w1_words, w1_scales, "e4m3")
    w2_ = mxq(f64(w2), 0, "e4m3")
    y = v[:, idx[0]].T @ w0_ + v[:, idx[1]].T @ w1_ + v[:, idx[2]].T @ w2_
    return y

from contextlib import ExitStack

import concourse.mybir as mybir

K, M, T, S = 1024, 256, 4096, 512
FLOPS = 2 * 3 * K * M * S

F32 = mybir.dt.float32
BF16 = mybir.dt.bfloat16
I32 = mybir.dt.int32
U32 = mybir.dt.uint32
U16 = mybir.dt.uint16
U8 = mybir.dt.uint8
FP8X4 = mybir.dt.float8_e4m3fn_x4
FP4X4 = mybir.dt.float4_e2m1fn_x4

P = 128
PACK = 4
K_PASS = P * PACK
PASSES = K // K_PASS
FIELDS = 3
QUADS = 4
QUAD = 32
BLOCKS = 16
LIST_COLS = S // 16
J_TILES = S // P
STAGE_ROW = 96


def tile_list_tabfield_tm_none_kernel(tc, tab, w0_words, w0_scales, w1_words, w1_scales, w2, offs, out):
    nc = tc.nc
    with ExitStack() as ctx:
        keep = ctx.enter_context(tc.tile_pool(name="keep", bufs=1))
        psum = ctx.enter_context(tc.psum_pool(name="psum", bufs=1))

        offsets = keep.tile([P, FIELDS * LIST_COLS], U16, name="offsets")
        scale_window = keep.tile([P, T], U8, name="scale_window", align_bytes=64)
        word_window = [keep.tile([P, T], I32, name="word_window%d" % a, align_bytes=64) for a in range(PASSES)]
        picked_scales = keep.tile([P, FIELDS * S], U8, name="picked_scales", align_bytes=64)
        table_plane = [keep.tile([P, FIELDS * S], U8, name="table_plane%d" % a, align_bytes=64) for a in range(PASSES)]
        w0_plane = keep.tile([P, PASSES, M], U8, name="w0_plane", align_bytes=64)
        w1_plane = keep.tile([P, PASSES, M], U8, name="w1_plane", align_bytes=64)
        w0_codes = keep.tile([P, PASSES, 2 * M], U8, name="w0_codes", align_bytes=64)
        w1_codes = [keep.tile([P, M], I32, name="w1_codes%d" % a, align_bytes=64) for a in range(PASSES)]
        w2_raw = [keep.tile([P, PACK, M], F32, name="w2_raw%d" % a, align_bytes=64) for a in range(PASSES)]
        w2_codes = [keep.tile([P, M], U32, name="w2_codes%d" % a, align_bytes=64) for a in range(PASSES)]
        w2_plane = [keep.tile([P, M], U8, name="w2_plane%d" % a, align_bytes=64) for a in range(PASSES)]
        acc = [psum.tile([P, M], F32, name="acc%d" % j) for j in range(J_TILES)]

        nc.vector.memset(w0_plane[:].rearrange("p a n -> p (a n)").bitcast(I32), 0)
        nc.vector.memset(w1_plane[:].rearrange("p a n -> p (a n)").bitcast(I32), 0)
        nc.vector.memset(scale_window[0:STAGE_ROW, :].bitcast(I32), 0)
        for a in range(PASSES):
            nc.vector.memset(table_plane[a][:].bitcast(I32), 0)

        def load_words(a):
            src = tab[a, 0 : K_PASS * T].rearrange("(p x) -> p x", p=P).bitcast(I32)
            nc.sync.dma_start(out=word_window[a][:], in_=src)

        def load_w1(a):
            nc.sync.dma_start(out=w1_codes[a][:], in_=w1_words[a].rearrange("p n i -> p (n i)").bitcast(I32))

        def load_w2(a):
            rows = w2[a * K_PASS : (a + 1) * K_PASS, :]
            nc.sync.dma_start(out=w2_raw[a][:], in_=rows.rearrange("(p i) n -> p i n", i=PACK))

        nc.sync.dma_start(offsets[:], offs)
        for a in range(PASSES):
            rows = tab[a, K_PASS * T :].rearrange("(q t) -> q t", q=BLOCKS).bitcast(I32)
            first = STAGE_ROW + BLOCKS * a
            nc.sync.dma_start(out=scale_window[first : first + BLOCKS, :].bitcast(I32), in_=rows)
        load_words(0)
        nc.sync.dma_start(out=w0_codes[:].bitcast(I32), in_=w0_words.rearrange("a p x -> p a x").bitcast(I32))
        load_w1(0)
        load_words(1)
        load_w2(0)
        load_w2(1)
        load_w1(1)

        for plane, scales in ((w0_plane, w0_scales), (w1_plane, w1_scales)):
            for quad in range(QUADS):
                rows = scales[:, 4 * quad : 4 * quad + 4, :].rearrange("a r n -> r a n").bitcast(I32)
                nc.gpsimd.dma_start(out=plane[QUAD * quad : QUAD * quad + 4, :, :].bitcast(I32), in_=rows)

        nc.vector.tensor_copy(picked_scales[:], scale_window[:].indirect(offsets[:]))
        for a, queue in ((0, nc.scalar), (1, nc.gpsimd)):
            for quad in range(QUADS):
                first = STAGE_ROW + BLOCKS * a + 4 * quad
                queue.dma_start(
                    out=table_plane[a][QUAD * quad : QUAD * quad + 4, :].bitcast(I32),
                    in_=picked_scales[first : first + 4, :].bitcast(I32),
                )

        def gather(a, f, tag):
            picked = keep.tile([P, S], U32, name="picked%d_%d" % (a, f), tag=tag, align_bytes=64)
            part = offsets[:, f * LIST_COLS : (f + 1) * LIST_COLS]
            nc.vector.tensor_copy(picked[:], word_window[a][:].bitcast(U32).indirect(part))
            return picked

        def quantize_w2(a):
            grouped = keep.tile([P, M, PACK], BF16, name="w2_grouped%d" % a, tag="grouped%d" % a, align_bytes=64)
            nc.scalar.copy(
                out=grouped[:].rearrange("p (c x) i -> p c i x", x=4),
                in_=w2_raw[a][:].rearrange("p i (c x) -> p c i x", x=4),
            )
            nc.vector.quantize_mx(
                out=w2_codes[a][:].bitcast(FP8X4), scales=w2_plane[a][:], in_=grouped[:].rearrange("p n i -> p (n i)")
            )

        def weight(a, f):
            if f == 0:
                return w0_codes[:, a, :].bitcast(FP4X4), w0_plane[:, a, :]
            if f == 1:
                return w1_codes[a][:].bitcast(FP8X4), w1_plane[:, a, :]
            return w2_codes[a][:].bitcast(FP8X4), w2_plane[a][:]

        def multiply(a, f, picked, start=False, stop=False):
            codes, plane = weight(a, f)
            for j in range(J_TILES):
                nc.tensor.matmul_mx(
                    out=acc[j][:],
                    lhsT=picked[:, j * P : (j + 1) * P].bitcast(FP8X4),
                    lhsT_scale=table_plane[a][:, f * S + j * P : f * S + (j + 1) * P],
                    rhs=codes,
                    rhs_scale=plane,
                    start=start,
                    stop=stop,
                )

        p00 = gather(0, 0, "picked00")
        p01 = gather(0, 1, "picked01")
        p02 = gather(0, 2, "picked02")
        multiply(0, 0, p00, start=True)
        multiply(0, 1, p01)
        p10 = gather(1, 0, "picked10")
        multiply(1, 0, p10)
        p11 = gather(1, 1, "picked11")
        multiply(1, 1, p11)
        quantize_w2(0)
        multiply(0, 2, p02)
        p12 = gather(1, 2, "grouped0")
        quantize_w2(1)
        multiply(1, 2, p12, stop=True)

        for j in range(J_TILES):
            result = keep.tile([P, M], F32, name="result%d" % j)
            if j % 2 == 0:
                nc.scalar.copy(out=result[:], in_=acc[j][:])
            else:
                nc.vector.tensor_copy(out=result[:], in_=acc[j][:])
            nc.sync.dma_start(out=out[j * P : (j + 1) * P, :], in_=result[:])
